import numpy as np, ml_dtypes
CORES = [4,12,20,28,44,60,76,84,92,108,116,124]
N = 12
KB, QP = 2, 256
MEM = [10]
def setup_inputs(rng):
    return {"q": rng.standard_normal((N, 128, QP), dtype=np.float32).astype(ml_dtypes.bfloat16), "k": rng.standard_normal((N, 128, KB * 128), dtype=np.float32).astype(ml_dtypes.bfloat16), "v": rng.standard_normal((N, 128, KB * 128), dtype=np.float32).astype(ml_dtypes.bfloat16)}
def setup_inputs_big(rng):
    d = setup_inputs(rng)
    for k in ("q", "k", "v"): d[k] = (d[k].astype(np.float32) * 1024.0).astype(d[k].dtype)
    return d
def setup_inputs_small(rng):
    d = setup_inputs(rng)
    for k in ("q", "k", "v"): d[k] = (d[k].astype(np.float32) * (1 / 1024.0)).astype(d[k].dtype)
    return d
def setup_inputs_apart(rng):
    d = setup_inputs(rng)
    f = (10.0 ** rng.permutation(np.linspace(-1.5, 1.5, N))).astype(np.float32).reshape(N, 1, 1)
    for k in ("q", "k", "v"): d[k] = (d[k].astype(np.float32) * f).astype(d[k].dtype)
    return d
def reference(q, k, v):
    Q, K, V = q.astype(np.float64), k.astype(np.float64), v.astype(np.float64)
    y = np.zeros((N, 128, QP))
    for r in range(N):
        for j in MEM:
            for b in range(KB):
                S = np.maximum(K[j][:, 128 * b:128 * b + 128].T @ Q[r], 0.0)
                y[r] += V[j][:, 128 * b:128 * b + 128].T @ S
    return {"y": y.astype(ml_dtypes.bfloat16 if q.dtype != np.float64 else np.float64)}

from concourse.bass import DstId, RemoteDMATransfer
from concourse.mybir import AluOpType

P, QP, KW = 128, 256, 256

SCRATCH = {
    "kd": ("dram", [P, KW], "bfloat16"),
    "vd": ("dram", [P, KW], "bfloat16"),
    "qb": ("sbuf", [P, QP], "bfloat16"),
    "kb": ("sbuf", [P, KW], "bfloat16"),
    "vb": ("sbuf", [P, KW], "bfloat16"),
    "zero": ("sbuf", [P, QP], "float32"),
    "s0": ("sbuf", [P, QP], "bfloat16"),
    "s1": ("sbuf", [P, QP], "bfloat16"),
    "yb": ("sbuf", [P, QP], "bfloat16"),
    "pa": ("psum", [P, 512], "float32"),
    "pb": ("psum", [P, 512], "float32"),
    "po": ("psum", [P, 512], "float32"),
}
SEMAPHORES = ["ldk", "ldv", "ldq", "karr", "varr", "left", "zs", "m0", "m1", "r0", "r1", "mo", "cy", "st"]


def _bits(mask):
    return [i for i in range(mask.bit_length()) if (mask >> i) & 1]


def _mask(engines):
    m = 0
    for e in engines:
        m |= 1 << e
    return m


def _common(topo, src, dests):
    m = topo.mask(src, dests[0])
    for d in dests[1:]:
        m &= topo.mask(src, d)
    return _bits(m)


def _plan(T, topo):
    owner = T.cores[T.tables["MEM"][0]]
    others = [c for c in T.cores if c != owner]
    near = [c for c in others if topo.may_write(owner, c)]
    far = [c for c in others if not topo.may_write(owner, c)]
    fwd = [c for c in range(topo.CHIPS * topo.CORES_PER_CHIP)
           if c != owner and topo.chip(c) == topo.chip(owner) and T.rank_of(c) is None
           and all(topo.may_write(c, d) for d in far)]
    same = [c for c in fwd if topo.die(c) == topo.die(owner)]
    cross = [c for c in fwd if topo.die(c) != topo.die(owner)]
    order = []
    for i in range(max(len(same), len(cross))):
        order += cross[i:i + 1] + same[i:i + 1]
    serve = dict((h, far[i::len(order)]) for i, h in enumerate(order))
    on = _common(topo, owner, order)
    off = _common(topo, owner, near)
    stay = [e for e in on if e not in off]
    n = len(order)
    kfeed = dict((h, on[i::n]) for i, h in enumerate(order))
    vfeed = dict((h, stay[i::n]) for i, h in enumerate(order))
    return owner, near, far, order, serve, off, kfeed, vfeed


def _send(g, topo, items, local_sem):
    trs = []
    for src_ap, dst_ap, dests, engines, sem in items:
        ids = []
        for d in dests:
            rid, pid, _ring = topo.addr(d)
            ids.append(DstId(rid=rid, pnc=pid))
        trs.append(RemoteDMATransfer(dst_ids=ids, dma_engine_mask=_mask(engines), remote_sem=sem,
                                     srcs=[src_ap], dsts=[dst_ap for _d in dests], alu_op=0))
    g.remote_dma_fused(trs, local_sem=local_sem)
    return sum(len(it[3]) for it in items)


def _attend(g, T, kcount, vcount):
    s = T.sem
    te, ve = g.tensor, g.vector
    ve.memset(T.zero[:], 0.0).then_inc(s.zs, 1)
    te.wait_ge(s.ldq, 16)
    te.wait_ge(s.karr, kcount)
    te.matmul(T.pa[:, 0:QP], T.kb[:, 0:128], T.qb[:], True, True).then_inc(s.m0, 1)
    te.matmul(T.pb[:, 0:QP], T.kb[:, 128:256], T.qb[:], True, True).then_inc(s.m1, 1)
    ve.wait_ge(s.zs, 1)
    ve.wait_ge(s.m0, 1)
    ve.tensor_tensor(T.s0[:], T.pa[:, 0:QP], T.zero[:], AluOpType.max).then_inc(s.r0, 1)
    ve.wait_ge(s.m1, 1)
    ve.tensor_tensor(T.s1[:], T.pb[:, 0:QP], T.zero[:], AluOpType.max).then_inc(s.r1, 1)
    te.wait_ge(s.varr, vcount)
    te.wait_ge(s.r0, 1)
    te.matmul(T.po[:, 0:QP], T.vb[:, 0:128], T.s0[:], True, False)
    te.wait_ge(s.r1, 1)
    te.matmul(T.po[:, 0:QP], T.vb[:, 128:256], T.s1[:], False, True).then_inc(s.mo, 1)
    ve.wait_ge(s.mo, 1)
    ve.tensor_copy(T.yb[:], T.po[:, 0:QP]).then_inc(s.cy, 1)
    g.sync.wait_ge(s.cy, 1)
    g.sync.dma_start(T.y[:], T.yb[:]).then_inc(s.st, 16)
    g.sync.wait_ge(s.st, 16)


def rank_program(g, core, T, topo):
    owner, near, far, order, serve, off, kfeed, vfeed = _plan(T, topo)
    s = T.sem

    if core == owner:
        g.sync.dma_start(T.kd[:], T.k[:]).then_inc(s.ldk, 16)
        g.scalar.dma_start(T.vd[:], T.v[:]).then_inc(s.ldv, 16)
        g.sync.dma_start(T.qb[:], T.q[:]).then_inc(s.ldq, 16)
        g.scalar.dma_start(T.kb[:], T.k[:]).then_inc(s.karr, 16)
        g.sync.dma_start(T.vb[:], T.v[:]).then_inc(s.varr, 16)
        g.wait_ge(s.ldk, 16)
        left = _send(g, topo, [(T.kd[:], T.kd[:], [h], kfeed[h], s.karr) for h in order], s.left)
        g.wait_ge(s.ldv, 16)
        left += _send(g, topo, [(T.vd[:], T.vd[:], [h], vfeed[h], s.varr) for h in order]
                      + [(T.kd[:], T.kb[:], near, off, s.karr)], s.left)
        left += _send(g, topo, [(T.vd[:], T.vb[:], near, off, s.varr)], s.left)
        _attend(g, T, 16, 16)
        g.wait_ge(s.left, left)
        return

    if core in serve:
        dests = serve[core]
        engines = _common(topo, core, dests)
        g.wait_ge(s.karr, len(kfeed[core]))
        left = _send(g, topo, [(T.kd[:], T.kb[:], dests, engines, s.karr)], s.left)
        g.wait_ge(s.varr, len(vfeed[core]))
        left += _send(g, topo, [(T.vd[:], T.vb[:], dests, engines, s.varr)], s.left)
        g.wait_ge(s.left, left)
        return

    if T.rank_of(core) is None:
        return

    g.sync.dma_start(T.qb[:], T.q[:]).then_inc(s.ldq, 16)
    if core in near:
        count = len(off)
    else:
        h = [c for c in order if core in serve[c]][0]
        count = len(_common(topo, h, serve[h]))
    _attend(g, T, count, count)
